import numpy as np
import ml_dtypes


def mxq(x, axis, fmt="e4m3"):
    dtype, down = {"e4m3": (ml_dtypes.float8_e4m3fn, 7), "e5m2": (ml_dtypes.float8_e5m2, 14)}[fmt]
    v = np.moveaxis(np.asarray(x, np.float32).astype(ml_dtypes.bfloat16).astype(np.float64), axis, -1)
    blocks = v.reshape(v.shape[:-1] + (-1, 32))
    amax = np.abs(blocks).max(-1, keepdims=True)
    byte = np.maximum(np.where(amax > 0, np.frexp(amax)[1] - 1 + 127, 0) - down, 1)
    scale = np.exp2(byte - 127.0)
    codes = (blocks / scale).astype(np.float32).astype(dtype).astype(np.float64)
    return np.moveaxis((codes * scale).reshape(v.shape), -1, axis)


WIDE = False


def mx_kscale(k):
    if not WIDE:
        return np.ones(k)
    levels = np.array([10, -10, 5, -5, 0])
    if k % 512:
        return np.exp2(np.random.permutation(np.resize(levels, k // 32))).repeat(32)
    a = np.empty((k // 512, 16))
    for p in range(k // 512):
        a[p, :8] = np.random.permutation(np.resize(levels, 8))
        for g in range(8):
            far = levels[np.abs(levels - a[p, g]) >= 10]
            a[p, g + 8] = far[np.random.randint(len(far))]
    return np.exp2(a.ravel()).repeat(32)


def f64(x):
    return np.asarray(x).astype(np.float64)


def striped(idx):
    return np.tile(idx.reshape(-1, 16).T, (8, 1)).astype(np.uint16)


def unstriped(offs):
    return offs[:16].T.reshape(-1).astype(np.int64)


E2M1 = np.array([0.0, 0.5, 1.0, 1.5, 2.0, 3.0, 4.0, 6.0, -0.0, -0.5, -1.0, -1.5, -2.0, -3.0, -4.0, -6.0])


def pack_weight(w, fmt):
    k, n = w.shape
    w = f64(np.asarray(w, np.float32).astype(ml_dtypes.bfloat16)).reshape(k // 32, 32, n)
    amax = np.abs(w).max(1)
    if fmt == "e4m3":
        byte = np.frexp(amax)[1] - 1 + 127 - 7
    else:
        mant, ex = np.frexp(amax / 6.0)
        byte = np.where(mant > 0.5, ex, ex - 1) + 127
    byte = np.clip(np.where(amax > 0, byte, 1), 1, 254)
    scaled = (w * np.exp2(127.0 - byte)[:, None, :]).reshape(k, n).astype(np.float32)
    by_word = np.ascontiguousarray(scaled.reshape(k // 512, 128, 4, n).transpose(0, 1, 3, 2))
    if fmt == "e4m3":
        words = by_word.astype(ml_dtypes.float8_e4m3fn).view(np.uint8)
    else:
        c = by_word.astype(ml_dtypes.float4_e2m1fn).view(np.uint8) & 0xF
        words = (c[..., 0::2] | (c[..., 1::2] << 4)).reshape(k // 512, 128, 2 * n)
    return np.ascontiguousarray(words), np.ascontiguousarray(byte.astype(np.uint8).reshape(k // 512, 16, n))


def unpack_weight(words, scales, fmt):
    g, _, n = scales.shape
    words = np.ascontiguousarray(words).reshape(g, 128, n, -1)
    if fmt == "e4m3":
        vals = words.view(ml_dtypes.float8_e4m3fn).astype(np.float64)
    else:
        nib = np.empty((g, 128, n, 4), np.uint8)
        nib[..., 0::2] = words & 0xF
        nib[..., 1::2] = words >> 4
        vals = E2M1[nib]
    vals = vals * np.repeat(np.exp2(scales.astype(np.float64) - 127.0), 8, axis=1)[..., None]
    return vals.transpose(0, 1, 3, 2).reshape(g * 512, n)


def gelu(v):
    return 0.5 * v * (1.0 + np.tanh(np.sqrt(2.0 / np.pi) * (v + 0.044715 * v**3)))


def striped8(idx):
    return np.concatenate([v.reshape(-1, 16).T for v in idx]).astype(np.uint16)


def unstriped8(offs):
    return np.stack([offs[16 * g:16 * g + 16].T.reshape(-1) for g in range(8)]).astype(np.int64)


def put_heads(h, wgs, idx8, t2):
    r = np.arange(h.shape[0])
    page = np.zeros((h.shape[0], t2))
    page[r[:, None], idx8[r % 512 // 64]] = wgs[r // 4 % 128] * h
    return page


def bf(x):
    return np.asarray(x, np.float32).astype(ml_dtypes.bfloat16)


def planes(Y):
    n, m = Y.shape
    b = f64(bf(Y)).reshape(n // 32, 32, m)
    amax = np.abs(b).max(1)
    byte = np.clip(np.where(amax > 0, np.frexp(amax)[1] - 1 + 127 - 7, 1), 1, 254)
    codes = (b * np.exp2(127.0 - byte)[:, None, :]).reshape(n, m).astype(np.float32).astype(ml_dtypes.float8_e4m3fn).view(np.uint8)
    words = codes.reshape(n // 512, 128, 4, m).transpose(0, 1, 3, 2)
    return np.ascontiguousarray(words), np.ascontiguousarray(byte.astype(np.uint8).reshape(n // 512, 16, m))


K, H, N, T, S, T2 = 1536, 1024, 512, 2048, 512, 1024

def setup_inputs():
    n = np.random.standard_normal
    s = mx_kscale(K)[:, None]
    u = mx_kscale(H)[:, None]
    tab_words, tab_scales = pack_weight(n((K, T)) * s, "e4m3")
    wt_words, wt_scales = pack_weight(n((K, H)) / np.sqrt(K) / s * u.T, "e2m1")
    wq_words, wq_scales = pack_weight(0.3 * n((H, N)) / np.sqrt(H) / (u * u), "e4m3")
    return {
        "tab_words": tab_words, "tab_scales": tab_scales,
        "offs": striped(np.random.permutation(T)[:S]),
        "wt_words": wt_words, "wt_scales": wt_scales,
        "wc": (n((K, H)) / np.sqrt(K) / s * u.T).astype(np.float32),
        "wgs": np.repeat(np.random.uniform(0.5, 2.0, (8, S)), 16, axis=0).astype(np.float32),
        "offs2": striped8(np.stack([np.random.permutation(T2)[:S] for _ in range(8)])),
        "base": (0.6 * n((H, T2)) * u).astype(np.float32),
        "wl": (n((H, N)) / np.sqrt(H) / u).astype(np.float32),
        "wq_words": wq_words, "wq_scales": wq_scales,
        "gain": np.exp(0.8 * n(N)).astype(np.float32),
    }

def reference(tab_words, tab_scales, offs, wt_words, wt_scales, wc, wgs, offs2, base, wl, wq_words, wq_scales, gain):
    v = unpack_weight(tab_words, tab_scales, "e4m3")[:, unstriped(offs)]
    wt = unpack_weight(wt_words, wt_scales, "e2m1")
    treated = wt.T @ v
    control = mxq(f64(wc), 0, "e4m3").T @ v
    h = treated - np.maximum(control, 0.0)
    page = put_heads(h, f64(wgs), unstriped8(offs2), T2)
    z = page + f64(base)
    z2 = np.square(z)
    wq = unpack_weight(wq_words, wq_scales, "e4m3")
    e = mxq(f64(wl), 0, "e4m3").T @ mxq(z, 0, "e4m3") + wq.T @ mxq(z2, 0, "e4m3")
    y = f64(gain)[:, None] / (1.0 + np.exp(-e))
    words, scales = planes(y)
    return y, words, scales

@@ -1,0 +1,290 @@
+from contextlib import ExitStack
+
+import concourse.mybir as mybir
+
+K, H, N, T, S, T2 = 1536, 1024, 512, 2048, 512, 1024
+FLOPS = 2 * (2 * K * H * S + 2 * H * N * T2)
+
+F32 = mybir.dt.float32
+BF16 = mybir.dt.bfloat16
+I32 = mybir.dt.int32
+U32 = mybir.dt.uint32
+U16 = mybir.dt.uint16
+U8 = mybir.dt.uint8
+FP8X4 = mybir.dt.float8_e4m3fn_x4
+FP4X4 = mybir.dt.float4_e2m1fn_x4
+ALU = mybir.AluOpType
+ACT = mybir.ActivationFunctionType
+
+P = 128
+PACK = 4
+PASS = P * PACK
+K_PASSES = K // PASS
+H_PASSES = H // PASS
+CHUNK = 256
+CHUNKS = T2 // CHUNK
+PAGES = 4
+
+
+def tile_list_coupon_uplift_cells_kernel(
+    tc, tab_words, tab_scales, offs, wt_words, wt_scales, wc, wgs, offs2, base, wl, wq_words, wq_scales, gain,
+    out_0, out_1, out_2,
+):
+    nc = tc.nc
+    with ExitStack() as ctx:
+        keep = ctx.enter_context(tc.tile_pool(name="keep", bufs=1))
+        ring = ctx.enter_context(tc.tile_pool(name="ring", bufs=1))
+        psum = ctx.enter_context(tc.psum_pool(name="psum", bufs=1))
+
+        picks = keep.tile([P, S // 16], U16, name="picks")
+        places = keep.tile([P, S // 16], U16, name="places")
+
+        def kept(shape, dtype, name):
+            return keep.tile(shape, dtype, name=name, align_bytes=64)
+
+        def bank(index, shape, name):
+            return psum.tile(shape, F32, name=name, tag="bank%d" % index)
+
+        def raw_slot(shape, name):
+            return ring.tile(shape, F32, name=name, tag="raw", bufs=4, align_bytes=64)
+
+        def load_scale_rows(queue, held, rows, passes):
+            by_row = rows.bitcast(I32).rearrange("a (q r) n -> r q a n", r=4)
+            view = held[:].bitcast(I32).rearrange("p (a n) -> p a n", a=passes)
+            for r in range(4):
+                queue.dma_start(out=view[r:P:32], in_=by_row[r])
+
+        tab_s = kept([P, K_PASSES * T], U8, "tab_s")
+        wt_s_raw = kept([P, K_PASSES * H], U8, "wt_s_raw")
+        wq_s_raw = kept([P, H_PASSES * N], U8, "wq_s_raw")
+        for held in (tab_s, wt_s_raw, wq_s_raw):
+            nc.vector.memset(held[:].bitcast(I32), 0)
+        pages = [kept([P, T2], F32, "page%d" % g) for g in range(PAGES)]
+        for page in pages:
+            nc.vector.memset(page[:], 0.0)
+
+
+        wt_raw = [kept([P, K_PASSES, 2 * PASS], U8, "wt_raw%d" % b) for b in range(H_PASSES)]
+        wt_by_p = wt_words.bitcast(I32).rearrange("a p n -> p a n")
+
+        def load_wt(b):
+            nc.sync.dma_start(out=wt_raw[b][:].bitcast(I32), in_=wt_by_p[:, :, b * 256:(b + 1) * 256])
+
+        def load_weight(rows, name):
+            raw = raw_slot([P, PACK, PASS], name)
+            nc.sync.dma_start(out=raw[:], in_=rows.rearrange("(p j) c -> p j c", j=PACK))
+            return raw
+
+        def load_wc(a, b):
+            return load_weight(wc[a * PASS:(a + 1) * PASS, b * PASS:(b + 1) * PASS], "wc_raw")
+
+        tab_w = [kept([P, T], U32, "tab_w%d" % a) for a in range(K_PASSES)]
+
+        def load_tab(a):
+            nc.sync.dma_start(out=tab_w[a][:].bitcast(I32), in_=tab_words[a].rearrange("p t i -> p (t i)").bitcast(I32))
+
+        def quantize_weight(raw, name):
+            rounded = ring.tile([P, PACK * PASS], BF16, name="rounded", tag="rounded", bufs=2, align_bytes=64)
+            nc.scalar.copy(
+                out=rounded[:].rearrange("p (i m j) -> p m j i", i=PACK, j=PACK),
+                in_=raw[:].rearrange("p j (m i) -> p m j i", i=PACK),
+            )
+            codes = kept([P, PASS], U32, name + "_c")
+            scales = kept([P, PASS], U8, name + "_s")
+            nc.vector.quantize_mx(out=codes[:].bitcast(FP8X4), scales=scales[:], in_=rounded[:])
+            return codes, scales
+
+        wt_w = [kept([P, K_PASSES, PACK, 2 * P], U8, "wt_w%d" % b) for b in range(H_PASSES)]
+        wt_s = kept([P, K_PASSES, H_PASSES, PACK, P], U8, "wt_s")
+
+        def deal_wt(b):
+            nc.vector.tensor_copy(
+                out=wt_w[b][:].bitcast(U16).rearrange("p a i m -> p a m i"),
+                in_=wt_raw[b][:].bitcast(U16).rearrange("p a (m i) -> p a m i", i=PACK),
+            )
+
+        wc_raw = {}
+        wc_raw[0, 0] = load_wc(0, 0)
+        load_scale_rows(nc.sync, tab_s, tab_scales, K_PASSES)
+        nc.sync.dma_start(picks[:], offs)
+        wc_raw[1, 0] = load_wc(1, 0)
+        load_scale_rows(nc.sync, wt_s_raw, wt_scales, K_PASSES)
+        load_wt(0)
+        load_tab(0)
+        wc_raw[2, 0] = load_wc(2, 0)
+        load_tab(1)
+        load_tab(2)
+        nc.sync.dma_start(places[:], offs2)
+        wgs_t = kept([P, S], F32, "wgs_t")
+        nc.sync.dma_start(out=wgs_t[:], in_=wgs)
+        load_wt(1)
+
+        deal_wt(0)
+        v_s = [kept([P, S], U8, "v_s%d" % a) for a in range(K_PASSES)]
+        for a in range(K_PASSES):
+            nc.vector.tensor_copy(v_s[a][:], tab_s[:, a * T:(a + 1) * T].indirect(picks[:]))
+        nc.vector.tensor_copy(
+            out=wt_s[:].rearrange("p a b i m -> p (a b) m i"),
+            in_=wt_s_raw[:].rearrange("p (g m i) -> p g m i", m=P, i=PACK),
+        )
+        v_w = [kept([P, S], U32, "v_w%d" % a) for a in range(K_PASSES)]
+        wc_q = {}
+        for a in range(K_PASSES):
+            wc_q[a, 0] = quantize_weight(wc_raw[a, 0], "wc%d0" % a)
+            nc.vector.tensor_copy(v_w[a][:], tab_w[a][:].indirect(picks[:]))
+
+        def stage_one_pass(b, a, i, control, treated):
+            flags = dict(start=(a == 0), stop=(a == K_PASSES - 1))
+            moving = dict(rhs=v_w[a][:].bitcast(FP8X4), rhs_scale=v_s[a][:])
+            codes, scales = wc_q[a, b]
+            cols = slice(i * P, (i + 1) * P)
+            nc.tensor.matmul_mx(out=control[:], lhsT=codes[:, cols].bitcast(FP8X4), lhsT_scale=scales[:, cols],
+                                **moving, **flags)
+            nc.tensor.matmul_mx(out=treated[:], lhsT=wt_w[b][:, a, i, :].bitcast(FP4X4),
+                                lhsT_scale=wt_s[:, a, b, i, :], **moving, **flags)
+
+        sums = {0: ([bank(2 * i, [P, S], "control") for i in range(PACK)],
+                    [bank(2 * i + 1, [P, S], "treated") for i in range(PACK)])}
+        for a in range(K_PASSES):
+            for i in range(PACK):
+                stage_one_pass(0, a, i, sums[0][0][i], sums[0][1][i])
+
+        def stage_one_slice(i):
+            sums[1][0].append(bank(2 * i, [P, S], "control"))
+            sums[1][1].append(bank(2 * i + 1, [P, S], "treated"))
+            for a in range(K_PASSES):
+                stage_one_pass(1, a, i, sums[1][0][i], sums[1][1][i])
+
+        deal_wt(1)
+
+        z = [kept([P, PACK, T2], F32, "z%d" % b) for b in range(H_PASSES)]
+
+        def load_base(b):
+            rows = base[b * PASS:(b + 1) * PASS, :].rearrange("(p i) m -> p i m", i=PACK)
+            for u in range(2):
+                nc.sync.dma_start(out=z[b][:, 2 * u:2 * u + 2, :], in_=rows[:, 2 * u:2 * u + 2, :])
+
+        load_base(0)
+        for a in range(K_PASSES):
+            wc_raw[a, 1] = load_wc(a, 1)
+        wl_raw = [load_weight(wl[b * PASS:(b + 1) * PASS, :], "wl_raw") for b in range(H_PASSES)]
+        wq_raw = kept([P, H_PASSES, N], I32, "wq_raw")
+        nc.sync.dma_start(out=wq_raw[:], in_=wq_words.rearrange("a p n i -> p a (n i)").bitcast(I32))
+        load_scale_rows(nc.sync, wq_s_raw, wq_scales, H_PASSES)
+        gain_t = kept([P, PACK], F32, "gain_t")
+        nc.sync.dma_start(out=gain_t[:], in_=gain.rearrange("(p t) -> p t", t=PACK))
+        load_base(1)
+
+        def uplift(b, i):
+            control, treated = sums[b]
+            rectified = ring.tile([P, S], F32, name="rectified", tag="rectified", bufs=2)
+            nc.scalar.activation(out=rectified[:], in_=control[i][:], func=ACT.Relu)
+            h = ring.tile([P, S], F32, name="h", tag="h", bufs=2)
+            nc.vector.tensor_tensor(h[:], treated[i][:], rectified[:], ALU.subtract)
+            weighted = ring.tile([P, S], F32, name="weighted", tag="weighted", bufs=3)
+            nc.gpsimd.tensor_tensor(weighted[:], h[:], wgs_t[:], ALU.mult)
+            return weighted
+
+        def put(b, i, h):
+            page = pages[(PACK * b + i) % PAGES]
+            nc.vector.tensor_copy(page[:].indirect(places[:]), h[:])
+
+        def add_base(engine, b, i, cols):
+            page = pages[(PACK * b + i) % PAGES]
+            engine.tensor_tensor(z[b][:, i, cols], page[:, cols], z[b][:, i, cols], ALU.add)
+
+        def quantize_cells(b, c, round_on_vector):
+            cols = slice(c * CHUNK, (c + 1) * CHUNK)
+            pair = ring.tile([P, 2, CHUNK * PACK], BF16, name="pair", tag="pair", bufs=3, align_bytes=64)
+            source = z[b][:, :, cols].rearrange("p i (g e) -> p g i e", e=4)
+            woven = [pair[:, s, :].rearrange("p (g e i) -> p g i e", e=4, i=PACK) for s in range(2)]
+            if round_on_vector:
+                nc.vector.tensor_copy(out=woven[0], in_=source)
+            else:
+                nc.scalar.copy(out=woven[0], in_=source)
+            nc.scalar.activation(out=woven[1], in_=source, func=ACT.Square)
+            codes = kept([P, 2 * CHUNK], U32, "z%d%d_c" % (b, c))
+            scales = kept([P, 2 * CHUNK], U8, "z%d%d_s" % (b, c))
+            nc.vector.quantize_mx(out=codes[:].bitcast(FP8X4), scales=scales[:],
+                                  in_=pair[:].rearrange("p s n -> p (s n)"))
+            return codes, scales
+
+        everything = slice(0, T2)
+        slices = [(b, i) for b in range(H_PASSES) for i in range(PACK)]
+        wq_w = kept([P, H_PASSES, PACK, P], I32, "wq_w")
+        wq_s = kept([P, H_PASSES, PACK, P], U8, "wq_s")
+        wl_q = []
+        z_q = {}
+        hs = [uplift(0, 0), uplift(0, 1)]
+        for n, (b, i) in enumerate(slices):
+            put(b, i, hs[n])
+            if n == 1:
+                for a in range(K_PASSES):
+                    wc_q[a, 1] = quantize_weight(wc_raw[a, 1], "wc%d1" % a)
+            if n == 2:
+                for g in range(H_PASSES):
+                    wl_q.append(quantize_weight(wl_raw[g], "wl%d" % g))
+                nc.vector.tensor_copy(out=wq_w[:].rearrange("p a t m -> p a m t"),
+                                      in_=wq_raw[:].rearrange("p a (m t) -> p a m t", t=PACK))
+                nc.vector.tensor_copy(out=wq_s[:].rearrange("p a t m -> p a m t"),
+                                      in_=wq_s_raw[:].rearrange("p (a m t) -> p a m t", m=P, t=PACK))
+            if n + 2 == PACK:
+                sums[1] = [], []
+            if n + 2 < len(slices):
+                if n + 2 >= PACK:
+                    stage_one_slice(n + 2 - PACK)
+                hs.append(uplift(*slices[n + 2]))
+            if n + 1 < len(slices):
+                add_base(nc.gpsimd, b, i, everything)
+            if n >= PACK:
+                z_q[0, n - PACK] = quantize_cells(0, n - PACK, False)
+
+        scores = [[bank(2 * c + u, [P, 2, CHUNK], "scores") for u in range(2)] for c in range(CHUNKS)]
+
+        def stage_two(b, c):
+            codes, scales = z_q[b, c]
+            wl_c, wl_s = wl_q[b]
+            for t in range(PACK):
+                cols = slice(t * P, (t + 1) * P)
+                stationary = [(wl_c[:, cols], wl_s[:, cols]), (wq_w[:, b, t, :], wq_s[:, b, t, :])]
+                for s in range(2):
+                    half = slice(s * CHUNK, (s + 1) * CHUNK)
+                    nc.tensor.matmul_mx(
+                        out=scores[c][t // 2][:, t % 2, :],
+                        lhsT=stationary[s][0].bitcast(FP8X4), lhsT_scale=stationary[s][1],
+                        rhs=codes[:, half].bitcast(FP8X4), rhs_scale=scales[:, half],
+                        start=(b == 0 and t % 2 == 0 and s == 0),
+                        stop=(b == H_PASSES - 1 and t % 2 == 1 and s == 1),
+                    )
+
+        for c in range(CHUNKS):
+            stage_two(0, c)
+
+        y_codes = kept([P, T2], U32, "y_codes")
+        y_scales = kept([P, T2], U8, "y_scales")
+        y_rows = out_0.rearrange("(p t) m -> p t m", t=PACK)
+        code_rows = out_1[0].rearrange("p m t -> p (m t)").bitcast(I32)
+
+        def finish(c):
+            cols = slice(c * CHUNK, (c + 1) * CHUNK)
+            y = raw_slot([P, PACK, CHUNK], "y")
+            for u in range(2):
+                nc.scalar.activation(out=y[:, 2 * u:2 * u + 2, :], in_=scores[c][u][:], func=ACT.Sigmoid)
+            for t in range(PACK):
+                nc.vector.tensor_scalar(y[:, t, :], y[:, t, :], gain_t[:, t:t + 1], None, ALU.mult)
+            nc.sync.dma_start(out=y_rows[:, :, cols], in_=y[:])
+            rounded = ring.tile([P, PACK * CHUNK], BF16, name="y_rounded", tag="rounded", bufs=2, align_bytes=64)
+            nc.vector.tensor_copy(out=rounded[:].rearrange("p (g e t) -> p g t e", e=4, t=PACK),
+                                  in_=y[:].rearrange("p t (g e) -> p g t e", e=4))
+            nc.vector.quantize_mx(out=y_codes[:, cols].bitcast(FP8X4), scales=y_scales[:, cols], in_=rounded[:])
+            nc.sync.dma_start(out=code_rows[:, cols], in_=y_codes[:, cols].bitcast(I32))
+
+        for c in range(CHUNKS):
+            add_base(nc.vector, 1, PACK - 1, slice(c * CHUNK, (c + 1) * CHUNK))
+            z_q[1, c] = quantize_cells(1, c, True)
+            stage_two(1, c)
+        for c in range(CHUNKS):
+            finish(c)
+        scale_rows = out_2[0].bitcast(I32).rearrange("(q r) n -> r q n", r=4)
+        for r in range(4):
+            nc.scalar.dma_start(out=scale_rows[r], in_=y_scales[:].bitcast(I32)[r:P:32])

@@ -1,6 +1,7 @@
 from contextlib import ExitStack
 
 import concourse.mybir as mybir
+from concourse.masks import make_identity
 
 K, H, N, T, S, T2 = 1536, 1024, 512, 2048, 512, 1024
 FLOPS = 2 * (2 * K * H * S + 2 * H * N * T2)
@@ -23,7 +24,10 @@ K_PASSES = K // PASS
 H_PASSES = H // PASS
 CHUNK = 256
 CHUNKS = T2 // CHUNK
-PAGES = 4
+GAINS_ON_SCALAR = 1
+ROUNDS_ON_SCALAR = 1
+LIVE_OPERANDS = 10
+PAGES = 7
 
 
 def tile_list_coupon_uplift_cells_kernel(
@@ -55,107 +59,149 @@ def tile_list_coupon_uplift_cells_kernel(
                 queue.dma_start(out=view[r:P:32], in_=by_row[r])
 
         tab_s = kept([P, K_PASSES * T], U8, "tab_s")
-        wt_s_raw = kept([P, K_PASSES * H], U8, "wt_s_raw")
+        wt_s = kept([P, K_PASSES * H], U8, "wt_s")
         wq_s_raw = kept([P, H_PASSES * N], U8, "wq_s_raw")
-        for held in (tab_s, wt_s_raw, wq_s_raw):
-            nc.vector.memset(held[:].bitcast(I32), 0)
+        nc.gpsimd.memset(tab_s[:, :2 * T].bitcast(I32), 0)
+        nc.vector.memset(tab_s[:, 2 * T:].bitcast(I32), 0)
+        nc.gpsimd.memset(wq_s_raw[:].bitcast(I32), 0)
         pages = [kept([P, T2], F32, "page%d" % g) for g in range(PAGES)]
-        for page in pages:
-            nc.vector.memset(page[:], 0.0)
+        for g, page in enumerate(pages):
+            (nc.vector if g < PACK else nc.gpsimd).memset(page[:], 0.0)
 
 
-        wt_raw = [kept([P, K_PASSES, 2 * PASS], U8, "wt_raw%d" % b) for b in range(H_PASSES)]
+        identity = kept([P, P], F32, "identity")
+        make_identity(nc, identity[:])
+
+        warm = kept([P, 16], F32, "warm")
+        nc.scalar.activation(out=warm[:, 0:1], in_=identity[:, 0:1], func=ACT.Sigmoid)
+
+        wt_w = [kept([P, K_PASSES, 2 * PASS], U8, "wt_w%d" % b) for b in range(H_PASSES)]
         wt_by_p = wt_words.bitcast(I32).rearrange("a p n -> p a n")
 
         def load_wt(b):
-            nc.sync.dma_start(out=wt_raw[b][:].bitcast(I32), in_=wt_by_p[:, :, b * 256:(b + 1) * 256])
+            nc.sync.dma_start(out=wt_w[b][:].bitcast(I32), in_=wt_by_p[:, :, b * 256:(b + 1) * 256])
 
         def load_weight(rows, name):
-            raw = raw_slot([P, PACK, PASS], name)
+            raw = raw_slot([P, PACK, rows.shape[1]], name)
             nc.sync.dma_start(out=raw[:], in_=rows.rearrange("(p j) c -> p j c", j=PACK))
             return raw
 
-        def load_wc(a, b):
-            return load_weight(wc[a * PASS:(a + 1) * PASS, b * PASS:(b + 1) * PASS], "wc_raw")
+        def load_wc(a, first, width):
+            return load_weight(wc[a * PASS:(a + 1) * PASS, first:first + width], "wc_raw")
 
         tab_w = [kept([P, T], U32, "tab_w%d" % a) for a in range(K_PASSES)]
 
         def load_tab(a):
             nc.sync.dma_start(out=tab_w[a][:].bitcast(I32), in_=tab_words[a].rearrange("p t i -> p (t i)").bitcast(I32))
 
-        def quantize_weight(raw, name):
-            rounded = ring.tile([P, PACK * PASS], BF16, name="rounded", tag="rounded", bufs=2, align_bytes=64)
-            nc.scalar.copy(
-                out=rounded[:].rearrange("p (i m j) -> p m j i", i=PACK, j=PACK),
-                in_=raw[:].rearrange("p j (m i) -> p m j i", i=PACK),
-            )
-            codes = kept([P, PASS], U32, name + "_c")
-            scales = kept([P, PASS], U8, name + "_s")
-            nc.vector.quantize_mx(out=codes[:].bitcast(FP8X4), scales=scales[:], in_=rounded[:])
+        def operand():
+            codes = ring.tile([P, PASS], U32, name="codes", tag="codes", bufs=LIVE_OPERANDS, align_bytes=64)
+            scales = ring.tile([P, PASS], U8, name="scales", tag="scales", bufs=LIVE_OPERANDS, align_bytes=64)
             return codes, scales
 
-        wt_w = [kept([P, K_PASSES, PACK, 2 * P], U8, "wt_w%d" % b) for b in range(H_PASSES)]
-        wt_s = kept([P, K_PASSES, H_PASSES, PACK, P], U8, "wt_s")
+        def quantize_columns(raw, codes, scales, dealt, copy, slot=("rounded", 2)):
+            rounded = ring.tile([P, PACK * raw.shape[2]], BF16, name="rounded", tag=slot[0], bufs=slot[1],
+                                align_bytes=64)
+            order = "p (i m j) -> p m j i" if dealt else "p (m i j) -> p m j i"
+            copy(out=rounded[:].rearrange(order, i=PACK, j=PACK), in_=raw[:].rearrange("p j (m i) -> p m j i", i=PACK))
+            nc.vector.quantize_mx(out=codes.bitcast(FP8X4), scales=scales, in_=rounded[:])
 
-        def deal_wt(b):
-            nc.vector.tensor_copy(
-                out=wt_w[b][:].bitcast(U16).rearrange("p a i m -> p a m i"),
-                in_=wt_raw[b][:].bitcast(U16).rearrange("p a (m i) -> p a m i", i=PACK),
-            )
+        def quantize_weight(raw, dealt, slot=("rounded", 2)):
+            codes, scales = operand()
+            quantize_columns(raw, codes[:], scales[:], dealt, nc.scalar.copy, slot)
+            return codes, scales
 
         wc_raw = {}
-        wc_raw[0, 0] = load_wc(0, 0)
-        load_scale_rows(nc.sync, tab_s, tab_scales, K_PASSES)
+        wc_raw[0, 0] = load_wc(0, 0, PASS)
         nc.sync.dma_start(picks[:], offs)
-        wc_raw[1, 0] = load_wc(1, 0)
-        load_scale_rows(nc.sync, wt_s_raw, wt_scales, K_PASSES)
-        load_wt(0)
+        load_scale_rows(nc.sync, wt_s, wt_scales, K_PASSES)
         load_tab(0)
-        wc_raw[2, 0] = load_wc(2, 0)
+        nc.sync.dma_start(places[:], offs2)
+        load_wt(0)
+        load_scale_rows(nc.sync, tab_s, tab_scales, K_PASSES)
+        wc_raw[1, 0] = load_wc(1, 0, PASS)
         load_tab(1)
         load_tab(2)
-        nc.sync.dma_start(places[:], offs2)
+        HALF = PASS // 2
+        wc_last = [load_wc(2, u * HALF, HALF) for u in range(2)]
         wgs_t = kept([P, S], F32, "wgs_t")
         nc.sync.dma_start(out=wgs_t[:], in_=wgs)
-        load_wt(1)
 
-        deal_wt(0)
         v_s = [kept([P, S], U8, "v_s%d" % a) for a in range(K_PASSES)]
         for a in range(K_PASSES):
             nc.vector.tensor_copy(v_s[a][:], tab_s[:, a * T:(a + 1) * T].indirect(picks[:]))
-        nc.vector.tensor_copy(
-            out=wt_s[:].rearrange("p a b i m -> p (a b) m i"),
-            in_=wt_s_raw[:].rearrange("p (g m i) -> p g m i", m=P, i=PACK),
-        )
         v_w = [kept([P, S], U32, "v_w%d" % a) for a in range(K_PASSES)]
         wc_q = {}
         for a in range(K_PASSES):
-            wc_q[a, 0] = quantize_weight(wc_raw[a, 0], "wc%d0" % a)
             nc.vector.tensor_copy(v_w[a][:], tab_w[a][:].indirect(picks[:]))
+            if a + 1 < K_PASSES:
+                wc_q[a, 0] = quantize_weight(wc_raw[a, 0], False)
+        halves = [slice(u * HALF, (u + 1) * HALF) for u in range(2)]
+        wc_q[2, 0] = operand()
+        for u in range(2):
+            quantize_columns(wc_last[u], wc_q[2, 0][0][:, halves[u]], wc_q[2, 0][1][:, halves[u]], False,
+                             nc.vector.tensor_copy)
 
-        def stage_one_pass(b, a, i, control, treated):
-            flags = dict(start=(a == 0), stop=(a == K_PASSES - 1))
-            moving = dict(rhs=v_w[a][:].bitcast(FP8X4), rhs_scale=v_s[a][:])
+        BLOCKS = S // P
+        whole = slice(0, PASS)
+
+        def shoppers(a, g):
+            cols = slice(g * P, (g + 1) * P)
+            return dict(lhsT=v_w[a][:, cols].bitcast(FP8X4), lhsT_scale=v_s[a][:, cols])
+
+        def control_pass(b, a, g, control, cols):
             codes, scales = wc_q[a, b]
-            cols = slice(i * P, (i + 1) * P)
-            nc.tensor.matmul_mx(out=control[:], lhsT=codes[:, cols].bitcast(FP8X4), lhsT_scale=scales[:, cols],
-                                **moving, **flags)
-            nc.tensor.matmul_mx(out=treated[:], lhsT=wt_w[b][:, a, i, :].bitcast(FP4X4),
-                                lhsT_scale=wt_s[:, a, b, i, :], **moving, **flags)
+            nc.tensor.matmul_mx(out=control[:, cols], rhs=codes[:, cols].bitcast(FP8X4), rhs_scale=scales[:, cols],
+                                start=(a == 0), stop=(a == K_PASSES - 1 and cols.stop == PASS), **shoppers(a, g))
 
-        sums = {0: ([bank(2 * i, [P, S], "control") for i in range(PACK)],
-                    [bank(2 * i + 1, [P, S], "treated") for i in range(PACK)])}
+        def treated_pass(b, a, g, treated):
+            first = a * H + b * PASS
+            nc.tensor.matmul_mx(out=treated[:], rhs=wt_w[b][:, a, :].bitcast(FP4X4),
+                                rhs_scale=wt_s[:, first:first + PASS],
+                                start=(a == 0), stop=(a == K_PASSES - 1), **shoppers(a, g))
+
+        def term_tile(g):
+            return ring.tile([P, 2, PACK, P], F32, name="terms", tag="terms%d" % g)
+
+        def by_slice(sums):
+            return sums[:].rearrange("j (p i) -> j i p", i=PACK)
+
+        def empty_treated(held, treated):
+            nc.scalar.activation(out=held[:, 0], in_=by_slice(treated), func=ACT.Copy, scale=-1.0)
+
+        def empty_control(held, control, on_vector):
+            if on_vector:
+                nc.vector.tensor_scalar(held[:, 1], by_slice(control), 0.0, None, ALU.max)
+            else:
+                nc.scalar.activation(out=held[:, 1], in_=by_slice(control), func=ACT.Relu)
+
+        sums = [(bank(2 * g + 1, [P, PASS], "control"), bank(2 * g, [P, PASS], "treated")) for g in range(BLOCKS)]
         for a in range(K_PASSES):
-            for i in range(PACK):
-                stage_one_pass(0, a, i, sums[0][0][i], sums[0][1][i])
+            for g in range(BLOCKS):
+                treated_pass(0, a, g, sums[g][1])
+                if a + 1 < K_PASSES:
+                    control_pass(0, a, g, sums[g][0], whole)
+        terms = {0: [term_tile(g) for g in range(BLOCKS)]}
+        for g in range(BLOCKS):
+            empty_treated(terms[0][g], sums[g][1])
+        for cols in halves:
+            for g in range(BLOCKS):
+                control_pass(0, K_PASSES - 1, g, sums[g][0], cols)
+        for g in range(BLOCKS):
+            empty_control(terms[0][g], sums[g][0], g % 2 == 1)
 
-        def stage_one_slice(i):
-            sums[1][0].append(bank(2 * i, [P, S], "control"))
-            sums[1][1].append(bank(2 * i + 1, [P, S], "treated"))
-            for a in range(K_PASSES):
-                stage_one_pass(1, a, i, sums[1][0][i], sums[1][1][i])
-
-        deal_wt(1)
+        def stage_one_second():
+            terms[1] = []
+            for g in range(BLOCKS):
+                spare = (1, 3, 4, 5, 6, 7)
+                control = bank(spare[2 * g % 6], [P, PASS], "control")
+                treated = bank(spare[2 * g % 6 + 1], [P, PASS], "treated")
+                for a in range(K_PASSES):
+                    treated_pass(1, a, g, treated)
+                    control_pass(1, a, g, control, whole)
+                terms[1].append(term_tile(g))
+                empty_treated(terms[1][g], treated)
+                empty_control(terms[1][g], control, False)
 
         z = [kept([P, PACK, T2], F32, "z%d" % b) for b in range(H_PASSES)]
 
@@ -164,80 +210,107 @@ def tile_list_coupon_uplift_cells_kernel(
             for u in range(2):
                 nc.sync.dma_start(out=z[b][:, 2 * u:2 * u + 2, :], in_=rows[:, 2 * u:2 * u + 2, :])
 
-        load_base(0)
+        load_wt(1)
         for a in range(K_PASSES):
-            wc_raw[a, 1] = load_wc(a, 1)
+            wc_raw[a, 1] = load_wc(a, PASS, PASS)
         wl_raw = [load_weight(wl[b * PASS:(b + 1) * PASS, :], "wl_raw") for b in range(H_PASSES)]
         wq_raw = kept([P, H_PASSES, N], I32, "wq_raw")
         nc.sync.dma_start(out=wq_raw[:], in_=wq_words.rearrange("a p n i -> p a (n i)").bitcast(I32))
         load_scale_rows(nc.sync, wq_s_raw, wq_scales, H_PASSES)
+        load_base(0)
         gain_t = kept([P, PACK], F32, "gain_t")
         nc.sync.dma_start(out=gain_t[:], in_=gain.rearrange("(p t) -> p t", t=PACK))
         load_base(1)
 
-        def uplift(b, i):
-            control, treated = sums[b]
-            rectified = ring.tile([P, S], F32, name="rectified", tag="rectified", bufs=2)
-            nc.scalar.activation(out=rectified[:], in_=control[i][:], func=ACT.Relu)
-            h = ring.tile([P, S], F32, name="h", tag="h", bufs=2)
-            nc.vector.tensor_tensor(h[:], treated[i][:], rectified[:], ALU.subtract)
-            weighted = ring.tile([P, S], F32, name="weighted", tag="weighted", bufs=3)
-            nc.gpsimd.tensor_tensor(weighted[:], h[:], wgs_t[:], ALU.mult)
-            return weighted
+        def uplift(b, i, slot=("h", 4)):
+            turned = bank(2 * (i % 2), [P, S], "turned")
+            for s in range(2):
+                for g in range(BLOCKS):
+                    nc.tensor.matmul(turned[:, g * P:(g + 1) * P], lhsT=terms[b][g][:, s, i, :], rhs=identity[:],
+                                     is_transpose=True, start=(g == 0 and s == 0), stop=(g == BLOCKS - 1 and s == 1))
+            h = ring.tile([P, S], F32, name="h", tag=slot[0], bufs=slot[1], align_bytes=64)
+            if b == 0 and i == 0:
+                nc.vector.tensor_scalar(h[:], turned[:], -1.0, None, ALU.mult)
+            else:
+                nc.scalar.activation(out=h[:], in_=turned[:], func=ACT.Copy, scale=-1.0)
+            return h
 
         def put(b, i, h):
             page = pages[(PACK * b + i) % PAGES]
-            nc.vector.tensor_copy(page[:].indirect(places[:]), h[:])
+            nc.vector.tensor_tensor(page[:].indirect(places[:]), h[:], wgs_t[:], ALU.mult)
 
         def add_base(engine, b, i, cols):
             page = pages[(PACK * b + i) % PAGES]
             engine.tensor_tensor(z[b][:, i, cols], page[:, cols], z[b][:, i, cols], ALU.add)
 
-        def quantize_cells(b, c, round_on_vector):
-            cols = slice(c * CHUNK, (c + 1) * CHUNK)
-            pair = ring.tile([P, 2, CHUNK * PACK], BF16, name="pair", tag="pair", bufs=3, align_bytes=64)
-            source = z[b][:, :, cols].rearrange("p i (g e) -> p g i e", e=4)
-            woven = [pair[:, s, :].rearrange("p (g e i) -> p g i e", e=4, i=PACK) for s in range(2)]
-            if round_on_vector:
-                nc.vector.tensor_copy(out=woven[0], in_=source)
-            else:
-                nc.scalar.copy(out=woven[0], in_=source)
-            nc.scalar.activation(out=woven[1], in_=source, func=ACT.Square)
-            codes = kept([P, 2 * CHUNK], U32, "z%d%d_c" % (b, c))
-            scales = kept([P, 2 * CHUNK], U8, "z%d%d_s" % (b, c))
+        def pair_tile():
+            return ring.tile([P, 2, CHUNK * PACK], BF16, name="pair", tag="pair", bufs=3, align_bytes=64)
+
+        def quantize_pair(pair):
+            codes, scales = operand()
             nc.vector.quantize_mx(out=codes[:].bitcast(FP8X4), scales=scales[:],
                                   in_=pair[:].rearrange("p s n -> p (s n)"))
             return codes, scales
 
+        def cells_by_vector(b, c, copy):
+            cols = slice(c * CHUNK, (c + 1) * CHUNK)
+            pair = pair_tile()
+            source = z[b][:, :, cols].rearrange("p i (g e) -> p g i e", e=4)
+            woven = [pair[:, s, :].rearrange("p (g e i) -> p g i e", e=4, i=PACK) for s in range(2)]
+            copy(out=woven[0], in_=source)
+            nc.scalar.activation(out=woven[1], in_=source, func=ACT.Square)
+            return quantize_pair(pair)
+
+        def cells_by_tensor(b, c):
+            pair = pair_tile()
+            words = pair[:].bitcast(F32)
+            for k in range(CHUNK // P):
+                block = c * (CHUNK // P) + k
+                cols = slice(block * P, (block + 1) * P)
+                summed = bank(block % 4, [P, PACK, P], "summed")
+                for i in range(PACK):
+                    for s, source in enumerate((z[b][:, i, cols], pages[(PACK * b + i) % PAGES][:, cols])):
+                        nc.tensor.matmul(summed[:, i, :], lhsT=source, rhs=identity[:], is_transpose=True,
+                                         start=(i == 0 and s == 0), stop=(i == PACK - 1 and s == 1))
+                rounded = ring.tile([P, 2, 2, P, 2], BF16, name="cell_words", tag="cell_words", bufs=2, align_bytes=64)
+                source = summed[:].rearrange("m (u e) p -> m u p e", e=2)
+                nc.scalar.copy(out=rounded[:, 0], in_=source)
+                nc.scalar.activation(out=rounded[:, 1], in_=source, func=ACT.Square)
+                back = bank(4 + block % 4, [P, 2, 2, P], "back")
+                as_words = rounded[:].rearrange("m s u p e -> m s u (p e)").bitcast(F32)
+                for s in range(2):
+                    for u in range(2):
+                        nc.tensor.transpose(back[:, s, u, :], as_words[:, s, u, :], identity[:])
+                nc.scalar.copy(out=words[:, :, k * 2 * P:(k + 1) * 2 * P].rearrange("p s (m u) -> p s m u", u=2),
+                               in_=back[:].rearrange("p s u m -> p s m u"))
+            return quantize_pair(pair)
+
         everything = slice(0, T2)
-        slices = [(b, i) for b in range(H_PASSES) for i in range(PACK)]
         wq_w = kept([P, H_PASSES, PACK, P], I32, "wq_w")
         wq_s = kept([P, H_PASSES, PACK, P], U8, "wq_s")
-        wl_q = []
         z_q = {}
-        hs = [uplift(0, 0), uplift(0, 1)]
-        for n, (b, i) in enumerate(slices):
-            put(b, i, hs[n])
-            if n == 1:
-                for a in range(K_PASSES):
-                    wc_q[a, 1] = quantize_weight(wc_raw[a, 1], "wc%d1" % a)
-            if n == 2:
-                for g in range(H_PASSES):
-                    wl_q.append(quantize_weight(wl_raw[g], "wl%d" % g))
-                nc.vector.tensor_copy(out=wq_w[:].rearrange("p a t m -> p a m t"),
-                                      in_=wq_raw[:].rearrange("p a (m t) -> p a m t", t=PACK))
-                nc.vector.tensor_copy(out=wq_s[:].rearrange("p a t m -> p a m t"),
-                                      in_=wq_s_raw[:].rearrange("p (a m t) -> p a m t", m=P, t=PACK))
-            if n + 2 == PACK:
-                sums[1] = [], []
-            if n + 2 < len(slices):
-                if n + 2 >= PACK:
-                    stage_one_slice(n + 2 - PACK)
-                hs.append(uplift(*slices[n + 2]))
-            if n + 1 < len(slices):
-                add_base(nc.gpsimd, b, i, everything)
-            if n >= PACK:
-                z_q[0, n - PACK] = quantize_cells(0, n - PACK, False)
+        for i in range(2):
+            put(0, i, uplift(0, i))
+        shared = ("shared", 1)
+        wc_q[0, 1] = quantize_weight(wc_raw[0, 1], False)
+        wc_q[1, 1] = quantize_weight(wc_raw[1, 1], False, shared)
+        wc_q[2, 1] = quantize_weight(wc_raw[2, 1], False)
+        put(0, 2, uplift(0, 2, shared))
+        put(0, 3, uplift(0, 3))
+        stage_one_second()
+        hs = [uplift(1, i) for i in range(PACK)]
+        wl_q = [quantize_weight(wl_raw[g], True) for g in range(H_PASSES)]
+        nc.vector.tensor_copy(out=wq_w[:].rearrange("p a t m -> p a m t"),
+                              in_=wq_raw[:].rearrange("p a (m t) -> p a m t", t=PACK))
+        nc.vector.tensor_copy(out=wq_s[:].rearrange("p a t m -> p a m t"),
+                              in_=wq_s_raw[:].rearrange("p (a m t) -> p a m t", m=P, t=PACK))
+        for i in range(PACK - 1):
+            put(1, i, hs[i])
+        for i in range(PACK - 1):
+            add_base(nc.vector, 1, i, everything)
+        for c in range(CHUNKS):
+            z_q[0, c] = cells_by_tensor(0, c)
+        put(1, PACK - 1, hs[PACK - 1])
 
         scores = [[bank(2 * c + u, [P, 2, CHUNK], "scores") for u in range(2)] for c in range(CHUNKS)]
 
@@ -271,7 +344,10 @@ def tile_list_coupon_uplift_cells_kernel(
             for u in range(2):
                 nc.scalar.activation(out=y[:, 2 * u:2 * u + 2, :], in_=scores[c][u][:], func=ACT.Sigmoid)
             for t in range(PACK):
-                nc.vector.tensor_scalar(y[:, t, :], y[:, t, :], gain_t[:, t:t + 1], None, ALU.mult)
+                if t < PACK - GAINS_ON_SCALAR:
+                    nc.vector.tensor_scalar(y[:, t, :], y[:, t, :], gain_t[:, t:t + 1], None, ALU.mult)
+                else:
+                    nc.scalar.activation(out=y[:, t, :], in_=y[:, t, :], func=ACT.Copy, scale=gain_t[:, t:t + 1])
             nc.sync.dma_start(out=y_rows[:, :, cols], in_=y[:])
             rounded = ring.tile([P, PACK * CHUNK], BF16, name="y_rounded", tag="rounded", bufs=2, align_bytes=64)
             nc.vector.tensor_copy(out=rounded[:].rearrange("p (g e t) -> p g t e", e=4, t=PACK),
@@ -281,7 +357,7 @@ def tile_list_coupon_uplift_cells_kernel(
 
         for c in range(CHUNKS):
             add_base(nc.vector, 1, PACK - 1, slice(c * CHUNK, (c + 1) * CHUNK))
-            z_q[1, c] = quantize_cells(1, c, True)
+            z_q[1, c] = cells_by_vector(1, c, nc.scalar.copy if c < ROUNDS_ON_SCALAR else nc.vector.tensor_copy)
             stage_two(1, c)
         for c in range(CHUNKS):
             finish(c)

@@ -49,8 +49,8 @@ def tile_list_coupon_uplift_cells_kernel(
         def bank(index, shape, name):
             return psum.tile(shape, F32, name=name, tag="bank%d" % index)
 
-        def raw_slot(shape, name):
-            return ring.tile(shape, F32, name=name, tag="raw", bufs=4, align_bytes=64)
+        def raw_slot(shape, name, slot=("raw", 3)):
+            return ring.tile(shape, F32, name=name, tag=slot[0], bufs=slot[1], align_bytes=64)
 
         def load_scale_rows(queue, held, rows, passes):
             by_row = rows.bitcast(I32).rearrange("a (q r) n -> r q a n", r=4)
@@ -59,8 +59,8 @@ def tile_list_coupon_uplift_cells_kernel(
                 queue.dma_start(out=view[r:P:32], in_=by_row[r])
 
         tab_s = kept([P, K_PASSES * T], U8, "tab_s")
-        wt_s = kept([P, K_PASSES * H], U8, "wt_s")
-        wq_s_raw = kept([P, H_PASSES * N], U8, "wq_s_raw")
+        wt_s = [kept([P, K_PASSES * PASS], U8, "wt_s%d" % b) for b in range(H_PASSES)]
+        wq_s_raw = kept([P, N], U8, "wq_s_raw")
         nc.gpsimd.memset(tab_s[:, :2 * T].bitcast(I32), 0)
         nc.vector.memset(tab_s[:, 2 * T:].bitcast(I32), 0)
         nc.gpsimd.memset(wq_s_raw[:].bitcast(I32), 0)
@@ -81,13 +81,13 @@ def tile_list_coupon_uplift_cells_kernel(
         def load_wt(b):
             nc.sync.dma_start(out=wt_w[b][:].bitcast(I32), in_=wt_by_p[:, :, b * 256:(b + 1) * 256])
 
-        def load_weight(rows, name):
-            raw = raw_slot([P, PACK, rows.shape[1]], name)
+        def load_weight(rows, name, slot=("raw", 3)):
+            raw = raw_slot([P, PACK, rows.shape[1]], name, slot)
             nc.sync.dma_start(out=raw[:], in_=rows.rearrange("(p j) c -> p j c", j=PACK))
             return raw
 
-        def load_wc(a, first, width):
-            return load_weight(wc[a * PASS:(a + 1) * PASS, first:first + width], "wc_raw")
+        def load_wc(a, first, width, slot=("raw", 3)):
+            return load_weight(wc[a * PASS:(a + 1) * PASS, first:first + width], "wc_raw", slot)
 
         tab_w = [kept([P, T], U32, "tab_w%d" % a) for a in range(K_PASSES)]
 
@@ -114,7 +114,7 @@ def tile_list_coupon_uplift_cells_kernel(
         wc_raw = {}
         wc_raw[0, 0] = load_wc(0, 0, PASS)
         nc.sync.dma_start(picks[:], offs)
-        load_scale_rows(nc.sync, wt_s, wt_scales, K_PASSES)
+        load_scale_rows(nc.sync, wt_s[0], wt_scales[:, :, :PASS], K_PASSES)
         load_tab(0)
         nc.sync.dma_start(places[:], offs2)
         load_wt(0)
@@ -123,9 +123,15 @@ def tile_list_coupon_uplift_cells_kernel(
         load_tab(1)
         load_tab(2)
         HALF = PASS // 2
-        wc_last = [load_wc(2, u * HALF, HALF) for u in range(2)]
+        shared = [("shared%d" % k, 1) for k in range(2)]
+        wc_last = [load_wc(2, 0, HALF, shared[0]), load_wc(2, HALF, HALF)]
         wgs_t = kept([P, S], F32, "wgs_t")
         nc.sync.dma_start(out=wgs_t[:], in_=wgs)
+        wq_raw = kept([P, H_PASSES, N], I32, "wq_raw")
+        nc.sync.dma_start(out=wq_raw[:], in_=wq_words.rearrange("a p n i -> p a (n i)").bitcast(I32))
+        for q in range(4):
+            nc.sync.dma_start(out=wq_s_raw[:].bitcast(I32)[32 * q:32 * q + 4 * H_PASSES],
+                              in_=wq_scales.bitcast(I32)[:, 4 * q:4 * q + 4, :])
 
         v_s = [kept([P, S], U8, "v_s%d" % a) for a in range(K_PASSES)]
         for a in range(K_PASSES):
@@ -137,7 +143,8 @@ def tile_list_coupon_uplift_cells_kernel(
             if a + 1 < K_PASSES:
                 wc_q[a, 0] = quantize_weight(wc_raw[a, 0], False)
         halves = [slice(u * HALF, (u + 1) * HALF) for u in range(2)]
-        wc_q[2, 0] = operand()
+        wc_q[2, 0] = (ring.tile([P, PASS], U32, name="last_codes", tag="wq0", align_bytes=64),
+                      ring.tile([P, PASS], U8, name="last_scales", tag="wq1", align_bytes=64))
         for u in range(2):
             quantize_columns(wc_last[u], wc_q[2, 0][0][:, halves[u]], wc_q[2, 0][1][:, halves[u]], False,
                              nc.vector.tensor_copy)
@@ -155,13 +162,12 @@ def tile_list_coupon_uplift_cells_kernel(
                                 start=(a == 0), stop=(a == K_PASSES - 1 and cols.stop == PASS), **shoppers(a, g))
 
         def treated_pass(b, a, g, treated):
-            first = a * H + b * PASS
             nc.tensor.matmul_mx(out=treated[:], rhs=wt_w[b][:, a, :].bitcast(FP4X4),
-                                rhs_scale=wt_s[:, first:first + PASS],
+                                rhs_scale=wt_s[b][:, a * PASS:(a + 1) * PASS],
                                 start=(a == 0), stop=(a == K_PASSES - 1), **shoppers(a, g))
 
         def term_tile(g):
-            return ring.tile([P, 2, PACK, P], F32, name="terms", tag="terms%d" % g)
+            return ring.tile([P, 2, PACK, P], F32, name="terms", tag="terms%d" % g, align_bytes=64)
 
         def by_slice(sums):
             return sums[:].rearrange("j (p i) -> j i p", i=PACK)
@@ -193,7 +199,7 @@ def tile_list_coupon_uplift_cells_kernel(
         def stage_one_second():
             terms[1] = []
             for g in range(BLOCKS):
-                spare = (1, 3, 4, 5, 6, 7)
+                spare = (0, 2, 4, 5, 6, 7)
                 control = bank(spare[2 * g % 6], [P, PASS], "control")
                 treated = bank(spare[2 * g % 6 + 1], [P, PASS], "treated")
                 for a in range(K_PASSES):
@@ -211,28 +217,24 @@ def tile_list_coupon_uplift_cells_kernel(
                 nc.sync.dma_start(out=z[b][:, 2 * u:2 * u + 2, :], in_=rows[:, 2 * u:2 * u + 2, :])
 
         load_wt(1)
-        for a in range(K_PASSES):
-            wc_raw[a, 1] = load_wc(a, PASS, PASS)
+        load_scale_rows(nc.sync, wt_s[1], wt_scales[:, :, PASS:], K_PASSES)
+        wc_raw[0, 1] = load_wc(0, PASS, PASS)
+        wc_raw[1, 1] = load_wc(1, PASS, PASS)
+        wc_raw[2, 1] = load_wc(2, PASS, PASS, shared[0])
         wl_raw = [load_weight(wl[b * PASS:(b + 1) * PASS, :], "wl_raw") for b in range(H_PASSES)]
-        wq_raw = kept([P, H_PASSES, N], I32, "wq_raw")
-        nc.sync.dma_start(out=wq_raw[:], in_=wq_words.rearrange("a p n i -> p a (n i)").bitcast(I32))
-        load_scale_rows(nc.sync, wq_s_raw, wq_scales, H_PASSES)
         load_base(0)
         gain_t = kept([P, PACK], F32, "gain_t")
         nc.sync.dma_start(out=gain_t[:], in_=gain.rearrange("(p t) -> p t", t=PACK))
         load_base(1)
 
         def uplift(b, i, slot=("h", 4)):
-            turned = bank(2 * (i % 2), [P, S], "turned")
+            turned = bank(2 * (i % 2) + 1, [P, S], "turned")
             for s in range(2):
                 for g in range(BLOCKS):
                     nc.tensor.matmul(turned[:, g * P:(g + 1) * P], lhsT=terms[b][g][:, s, i, :], rhs=identity[:],
                                      is_transpose=True, start=(g == 0 and s == 0), stop=(g == BLOCKS - 1 and s == 1))
             h = ring.tile([P, S], F32, name="h", tag=slot[0], bufs=slot[1], align_bytes=64)
-            if b == 0 and i == 0:
-                nc.vector.tensor_scalar(h[:], turned[:], -1.0, None, ALU.mult)
-            else:
-                nc.scalar.activation(out=h[:], in_=turned[:], func=ACT.Copy, scale=-1.0)
+            nc.scalar.activation(out=h[:], in_=turned[:], func=ACT.Copy, scale=-1.0)
             return h
 
         def put(b, i, h):
@@ -286,24 +288,24 @@ def tile_list_coupon_uplift_cells_kernel(
             return quantize_pair(pair)
 
         everything = slice(0, T2)
-        wq_w = kept([P, H_PASSES, PACK, P], I32, "wq_w")
-        wq_s = kept([P, H_PASSES, PACK, P], U8, "wq_s")
+        wq_s = kept([P, PACK, P], U8, "wq_s")
+        wq_w = [ring.tile([P, PACK, P], I32, name="wq_w", tag="wq%d" % g, align_bytes=64) for g in range(H_PASSES)]
+        for g in range(H_PASSES):
+            nc.vector.tensor_copy(out=wq_w[g][:].rearrange("p t m -> p m t"),
+                                  in_=wq_raw[:, g, :].rearrange("p (m t) -> p m t", t=PACK))
+        nc.vector.tensor_copy(out=wq_s[:].rearrange("p t m -> p m t"),
+                              in_=wq_s_raw[:].rearrange("p (m t) -> p m t", t=PACK))
         z_q = {}
         for i in range(2):
             put(0, i, uplift(0, i))
-        shared = ("shared", 1)
         wc_q[0, 1] = quantize_weight(wc_raw[0, 1], False)
-        wc_q[1, 1] = quantize_weight(wc_raw[1, 1], False, shared)
-        wc_q[2, 1] = quantize_weight(wc_raw[2, 1], False)
-        put(0, 2, uplift(0, 2, shared))
-        put(0, 3, uplift(0, 3))
+        wc_q[1, 1] = quantize_weight(wc_raw[1, 1], False)
+        wc_q[2, 1] = quantize_weight(wc_raw[2, 1], False, shared[1])
+        put(0, 2, uplift(0, 2, shared[0]))
+        put(0, 3, uplift(0, 3, shared[1]))
         stage_one_second()
         hs = [uplift(1, i) for i in range(PACK)]
-        wl_q = [quantize_weight(wl_raw[g], True) for g in range(H_PASSES)]
-        nc.vector.tensor_copy(out=wq_w[:].rearrange("p a t m -> p a m t"),
-                              in_=wq_raw[:].rearrange("p a (m t) -> p a m t", t=PACK))
-        nc.vector.tensor_copy(out=wq_s[:].rearrange("p a t m -> p a m t"),
-                              in_=wq_s_raw[:].rearrange("p (a m t) -> p a m t", m=P, t=PACK))
+        wl_q = [quantize_weight(wl_raw[0], True, ("terms0", 1))]
         for i in range(PACK - 1):
             put(1, i, hs[i])
         for i in range(PACK - 1):
@@ -311,6 +313,7 @@ def tile_list_coupon_uplift_cells_kernel(
         for c in range(CHUNKS):
             z_q[0, c] = cells_by_tensor(0, c)
         put(1, PACK - 1, hs[PACK - 1])
+        wl_q.append(quantize_weight(wl_raw[1], True, ("terms1", 1)))
 
         scores = [[bank(2 * c + u, [P, 2, CHUNK], "scores") for u in range(2)] for c in range(CHUNKS)]
 
@@ -319,7 +322,7 @@ def tile_list_coupon_uplift_cells_kernel(
             wl_c, wl_s = wl_q[b]
             for t in range(PACK):
                 cols = slice(t * P, (t + 1) * P)
-                stationary = [(wl_c[:, cols], wl_s[:, cols]), (wq_w[:, b, t, :], wq_s[:, b, t, :])]
+                stationary = [(wl_c[:, cols], wl_s[:, cols]), (wq_w[b][:, t, :], wq_s[4 * b:, t, :])]
                 for s in range(2):
                     half = slice(s * CHUNK, (s + 1) * CHUNK)
                     nc.tensor.matmul_mx(
@@ -340,7 +343,7 @@ def tile_list_coupon_uplift_cells_kernel(
 
         def finish(c):
             cols = slice(c * CHUNK, (c + 1) * CHUNK)
-            y = raw_slot([P, PACK, CHUNK], "y")
+            y = raw_slot([P, PACK, CHUNK], "y", ("raw", 3) if c < 3 else shared[0])
             for u in range(2):
                 nc.scalar.activation(out=y[:, 2 * u:2 * u + 2, :], in_=scores[c][u][:], func=ACT.Sigmoid)
             for t in range(PACK):

@@ -72,9 +72,6 @@ def tile_list_coupon_uplift_cells_kernel(
         identity = kept([P, P], F32, "identity")
         make_identity(nc, identity[:])
 
-        warm = kept([P, 16], F32, "warm")
-        nc.scalar.activation(out=warm[:, 0:1], in_=identity[:, 0:1], func=ACT.Sigmoid)
-
         wt_w = [kept([P, K_PASSES, 2 * PASS], U8, "wt_w%d" % b) for b in range(H_PASSES)]
         wt_by_p = wt_words.bitcast(I32).rearrange("a p n -> p a n")
 
@@ -129,9 +126,6 @@ def tile_list_coupon_uplift_cells_kernel(
         nc.sync.dma_start(out=wgs_t[:], in_=wgs)
         wq_raw = kept([P, H_PASSES, N], I32, "wq_raw")
         nc.sync.dma_start(out=wq_raw[:], in_=wq_words.rearrange("a p n i -> p a (n i)").bitcast(I32))
-        for q in range(4):
-            nc.sync.dma_start(out=wq_s_raw[:].bitcast(I32)[32 * q:32 * q + 4 * H_PASSES],
-                              in_=wq_scales.bitcast(I32)[:, 4 * q:4 * q + 4, :])
 
         v_s = [kept([P, S], U8, "v_s%d" % a) for a in range(K_PASSES)]
         for a in range(K_PASSES):
@@ -217,14 +211,17 @@ def tile_list_coupon_uplift_cells_kernel(
                 nc.sync.dma_start(out=z[b][:, 2 * u:2 * u + 2, :], in_=rows[:, 2 * u:2 * u + 2, :])
 
         load_wt(1)
-        load_scale_rows(nc.sync, wt_s[1], wt_scales[:, :, PASS:], K_PASSES)
         wc_raw[0, 1] = load_wc(0, PASS, PASS)
         wc_raw[1, 1] = load_wc(1, PASS, PASS)
         wc_raw[2, 1] = load_wc(2, PASS, PASS, shared[0])
-        wl_raw = [load_weight(wl[b * PASS:(b + 1) * PASS, :], "wl_raw") for b in range(H_PASSES)]
-        load_base(0)
+        load_scale_rows(nc.sync, wt_s[1], wt_scales[:, :, PASS:], K_PASSES)
+        for q in range(4):
+            nc.sync.dma_start(out=wq_s_raw[:].bitcast(I32)[32 * q:32 * q + 4 * H_PASSES],
+                              in_=wq_scales.bitcast(I32)[:, 4 * q:4 * q + 4, :])
         gain_t = kept([P, PACK], F32, "gain_t")
         nc.sync.dma_start(out=gain_t[:], in_=gain.rearrange("(p t) -> p t", t=PACK))
+        wl_raw = [load_weight(wl[b * PASS:(b + 1) * PASS, :], "wl_raw") for b in range(H_PASSES)]
+        load_base(0)
         load_base(1)
 
         def uplift(b, i, slot=("h", 4)):

@@ -72,6 +72,9 @@ def tile_list_coupon_uplift_cells_kernel(
         identity = kept([P, P], F32, "identity")
         make_identity(nc, identity[:])
 
+        warm = kept([P, 16], F32, "warm")
+        nc.scalar.activation(out=warm[:, 0:1], in_=identity[:, 0:1], func=ACT.Sigmoid)
+
         wt_w = [kept([P, K_PASSES, 2 * PASS], U8, "wt_w%d" % b) for b in range(H_PASSES)]
         wt_by_p = wt_words.bitcast(I32).rearrange("a p n -> p a n")
 

from contextlib import ExitStack

import concourse.mybir as mybir
from concourse.masks import make_identity

K, H, N, T, S, T2 = 1536, 1024, 512, 2048, 512, 1024
FLOPS = 2 * (2 * K * H * S + 2 * H * N * T2)

F32 = mybir.dt.float32
BF16 = mybir.dt.bfloat16
I32 = mybir.dt.int32
U32 = mybir.dt.uint32
U16 = mybir.dt.uint16
U8 = mybir.dt.uint8
FP8X4 = mybir.dt.float8_e4m3fn_x4
FP4X4 = mybir.dt.float4_e2m1fn_x4
ALU = mybir.AluOpType
ACT = mybir.ActivationFunctionType

P = 128
PACK = 4
PASS = P * PACK
K_PASSES = K // PASS
H_PASSES = H // PASS
CHUNK = 256
CHUNKS = T2 // CHUNK
GAINS_ON_SCALAR = 1
ROUNDS_ON_SCALAR = 1
LIVE_OPERANDS = 10
PAGES = 7


def tile_list_coupon_uplift_cells_kernel(
    tc, tab_words, tab_scales, offs, wt_words, wt_scales, wc, wgs, offs2, base, wl, wq_words, wq_scales, gain,
    out_0, out_1, out_2,
):
    nc = tc.nc
    with ExitStack() as ctx:
        keep = ctx.enter_context(tc.tile_pool(name="keep", bufs=1))
        ring = ctx.enter_context(tc.tile_pool(name="ring", bufs=1))
        psum = ctx.enter_context(tc.psum_pool(name="psum", bufs=1))

        picks = keep.tile([P, S // 16], U16, name="picks")
        places = keep.tile([P, S // 16], U16, name="places")

        def kept(shape, dtype, name):
            return keep.tile(shape, dtype, name=name, align_bytes=64)

        def bank(index, shape, name):
            return psum.tile(shape, F32, name=name, tag="bank%d" % index)

        def raw_slot(shape, name, slot=("raw", 3)):
            return ring.tile(shape, F32, name=name, tag=slot[0], bufs=slot[1], align_bytes=64)

        def load_scale_rows(queue, held, rows, passes):
            by_row = rows.bitcast(I32).rearrange("a (q r) n -> r q a n", r=4)
            view = held[:].bitcast(I32).rearrange("p (a n) -> p a n", a=passes)
            for r in range(4):
                queue.dma_start(out=view[r:P:32], in_=by_row[r])

        tab_s = kept([P, K_PASSES * T], U8, "tab_s")
        wt_s = [kept([P, K_PASSES * PASS], U8, "wt_s%d" % b) for b in range(H_PASSES)]
        wq_s_raw = kept([P, N], U8, "wq_s_raw")
        nc.gpsimd.memset(tab_s[:, :2 * T].bitcast(I32), 0)
        nc.vector.memset(tab_s[:, 2 * T:].bitcast(I32), 0)
        nc.gpsimd.memset(wq_s_raw[:].bitcast(I32), 0)
        pages = [kept([P, T2], F32, "page%d" % g) for g in range(PAGES)]
        for g, page in enumerate(pages):
            (nc.vector if g < PACK else nc.gpsimd).memset(page[:], 0.0)


        identity = kept([P, P], F32, "identity")
        make_identity(nc, identity[:])

        warm = kept([P, 16], F32, "warm")
        nc.scalar.activation(out=warm[:, 0:1], in_=identity[:, 0:1], func=ACT.Sigmoid)

        wt_w = [kept([P, K_PASSES, 2 * PASS], U8, "wt_w%d" % b) for b in range(H_PASSES)]
        wt_by_p = wt_words.bitcast(I32).rearrange("a p n -> p a n")

        def load_wt(b):
            nc.sync.dma_start(out=wt_w[b][:].bitcast(I32), in_=wt_by_p[:, :, b * 256:(b + 1) * 256])

        def load_weight(rows, name, slot=("raw", 3)):
            raw = raw_slot([P, PACK, rows.shape[1]], name, slot)
            nc.sync.dma_start(out=raw[:], in_=rows.rearrange("(p j) c -> p j c", j=PACK))
            return raw

        def load_wc(a, first, width, slot=("raw", 3)):
            return load_weight(wc[a * PASS:(a + 1) * PASS, first:first + width], "wc_raw", slot)

        tab_w = [kept([P, T], U32, "tab_w%d" % a) for a in range(K_PASSES)]

        def load_tab(a):
            nc.sync.dma_start(out=tab_w[a][:].bitcast(I32), in_=tab_words[a].rearrange("p t i -> p (t i)").bitcast(I32))

        def operand():
            codes = ring.tile([P, PASS], U32, name="codes", tag="codes", bufs=LIVE_OPERANDS, align_bytes=64)
            scales = ring.tile([P, PASS], U8, name="scales", tag="scales", bufs=LIVE_OPERANDS, align_bytes=64)
            return codes, scales

        def quantize_columns(raw, codes, scales, dealt, copy, slot=("rounded", 2)):
            rounded = ring.tile([P, PACK * raw.shape[2]], BF16, name="rounded", tag=slot[0], bufs=slot[1],
                                align_bytes=64)
            order = "p (i m j) -> p m j i" if dealt else "p (m i j) -> p m j i"
            copy(out=rounded[:].rearrange(order, i=PACK, j=PACK), in_=raw[:].rearrange("p j (m i) -> p m j i", i=PACK))
            nc.vector.quantize_mx(out=codes.bitcast(FP8X4), scales=scales, in_=rounded[:])

        def quantize_weight(raw, dealt, slot=("rounded", 2)):
            codes, scales = operand()
            quantize_columns(raw, codes[:], scales[:], dealt, nc.scalar.copy, slot)
            return codes, scales

        wc_raw = {}
        wc_raw[0, 0] = load_wc(0, 0, PASS)
        nc.sync.dma_start(picks[:], offs)
        load_scale_rows(nc.sync, wt_s[0], wt_scales[:, :, :PASS], K_PASSES)
        load_tab(0)
        nc.sync.dma_start(places[:], offs2)
        load_wt(0)
        load_scale_rows(nc.sync, tab_s, tab_scales, K_PASSES)
        wc_raw[1, 0] = load_wc(1, 0, PASS)
        load_tab(1)
        load_tab(2)
        HALF = PASS // 2
        shared = [("shared%d" % k, 1) for k in range(2)]
        wc_last = [load_wc(2, 0, HALF, shared[0]), load_wc(2, HALF, HALF)]
        wgs_t = kept([P, S], F32, "wgs_t")
        nc.sync.dma_start(out=wgs_t[:], in_=wgs)
        wq_raw = kept([P, H_PASSES, N], I32, "wq_raw")
        nc.sync.dma_start(out=wq_raw[:], in_=wq_words.rearrange("a p n i -> p a (n i)").bitcast(I32))

        v_s = [kept([P, S], U8, "v_s%d" % a) for a in range(K_PASSES)]
        for a in range(K_PASSES):
            nc.vector.tensor_copy(v_s[a][:], tab_s[:, a * T:(a + 1) * T].indirect(picks[:]))
        v_w = [kept([P, S], U32, "v_w%d" % a) for a in range(K_PASSES)]
        wc_q = {}
        for a in range(K_PASSES):
            nc.vector.tensor_copy(v_w[a][:], tab_w[a][:].indirect(picks[:]))
            if a + 1 < K_PASSES:
                wc_q[a, 0] = quantize_weight(wc_raw[a, 0], False)
        halves = [slice(u * HALF, (u + 1) * HALF) for u in range(2)]
        wc_q[2, 0] = (ring.tile([P, PASS], U32, name="last_codes", tag="wq0", align_bytes=64),
                      ring.tile([P, PASS], U8, name="last_scales", tag="wq1", align_bytes=64))
        for u in range(2):
            quantize_columns(wc_last[u], wc_q[2, 0][0][:, halves[u]], wc_q[2, 0][1][:, halves[u]], False,
                             nc.vector.tensor_copy)

        BLOCKS = S // P
        whole = slice(0, PASS)

        def shoppers(a, g):
            cols = slice(g * P, (g + 1) * P)
            return dict(lhsT=v_w[a][:, cols].bitcast(FP8X4), lhsT_scale=v_s[a][:, cols])

        def control_pass(b, a, g, control, cols):
            codes, scales = wc_q[a, b]
            nc.tensor.matmul_mx(out=control[:, cols], rhs=codes[:, cols].bitcast(FP8X4), rhs_scale=scales[:, cols],
                                start=(a == 0), stop=(a == K_PASSES - 1 and cols.stop == PASS), **shoppers(a, g))

        def treated_pass(b, a, g, treated):
            nc.tensor.matmul_mx(out=treated[:], rhs=wt_w[b][:, a, :].bitcast(FP4X4),
                                rhs_scale=wt_s[b][:, a * PASS:(a + 1) * PASS],
                                start=(a == 0), stop=(a == K_PASSES - 1), **shoppers(a, g))

        def term_tile(g):
            return ring.tile([P, 2, PACK, P], F32, name="terms", tag="terms%d" % g, align_bytes=64)

        def by_slice(sums):
            return sums[:].rearrange("j (p i) -> j i p", i=PACK)

        def empty_treated(held, treated):
            nc.scalar.activation(out=held[:, 0], in_=by_slice(treated), func=ACT.Copy, scale=-1.0)

        def empty_control(held, control, on_vector):
            if on_vector:
                nc.vector.tensor_scalar(held[:, 1], by_slice(control), 0.0, None, ALU.max)
            else:
                nc.scalar.activation(out=held[:, 1], in_=by_slice(control), func=ACT.Relu)

        sums = [(bank(2 * g + 1, [P, PASS], "control"), bank(2 * g, [P, PASS], "treated")) for g in range(BLOCKS)]
        for a in range(K_PASSES):
            for g in range(BLOCKS):
                treated_pass(0, a, g, sums[g][1])
                if a + 1 < K_PASSES:
                    control_pass(0, a, g, sums[g][0], whole)
        terms = {0: [term_tile(g) for g in range(BLOCKS)]}
        for g in range(BLOCKS):
            empty_treated(terms[0][g], sums[g][1])
        for cols in halves:
            for g in range(BLOCKS):
                control_pass(0, K_PASSES - 1, g, sums[g][0], cols)
        for g in range(BLOCKS):
            empty_control(terms[0][g], sums[g][0], g % 2 == 1)

        def stage_one_second():
            terms[1] = []
            for g in range(BLOCKS):
                spare = (0, 2, 4, 5, 6, 7)
                control = bank(spare[2 * g % 6], [P, PASS], "control")
                treated = bank(spare[2 * g % 6 + 1], [P, PASS], "treated")
                for a in range(K_PASSES):
                    treated_pass(1, a, g, treated)
                    control_pass(1, a, g, control, whole)
                terms[1].append(term_tile(g))
                empty_treated(terms[1][g], treated)
                empty_control(terms[1][g], control, False)

        z = [kept([P, PACK, T2], F32, "z%d" % b) for b in range(H_PASSES)]

        def load_base(b):
            rows = base[b * PASS:(b + 1) * PASS, :].rearrange("(p i) m -> p i m", i=PACK)
            for u in range(2):
                nc.sync.dma_start(out=z[b][:, 2 * u:2 * u + 2, :], in_=rows[:, 2 * u:2 * u + 2, :])

        load_wt(1)
        wc_raw[0, 1] = load_wc(0, PASS, PASS)
        wc_raw[1, 1] = load_wc(1, PASS, PASS)
        wc_raw[2, 1] = load_wc(2, PASS, PASS, shared[0])
        load_scale_rows(nc.sync, wt_s[1], wt_scales[:, :, PASS:], K_PASSES)
        for q in range(4):
            nc.sync.dma_start(out=wq_s_raw[:].bitcast(I32)[32 * q:32 * q + 4 * H_PASSES],
                              in_=wq_scales.bitcast(I32)[:, 4 * q:4 * q + 4, :])
        gain_t = kept([P, PACK], F32, "gain_t")
        nc.sync.dma_start(out=gain_t[:], in_=gain.rearrange("(p t) -> p t", t=PACK))
        wl_raw = [load_weight(wl[b * PASS:(b + 1) * PASS, :], "wl_raw") for b in range(H_PASSES)]
        load_base(0)
        load_base(1)

        def uplift(b, i, slot=("h", 4)):
            turned = bank(2 * (i % 2) + 1, [P, S], "turned")
            for s in range(2):
                for g in range(BLOCKS):
                    nc.tensor.matmul(turned[:, g * P:(g + 1) * P], lhsT=terms[b][g][:, s, i, :], rhs=identity[:],
                                     is_transpose=True, start=(g == 0 and s == 0), stop=(g == BLOCKS - 1 and s == 1))
            h = ring.tile([P, S], F32, name="h", tag=slot[0], bufs=slot[1], align_bytes=64)
            nc.scalar.activation(out=h[:], in_=turned[:], func=ACT.Copy, scale=-1.0)
            return h

        def put(b, i, h):
            page = pages[(PACK * b + i) % PAGES]
            nc.vector.tensor_tensor(page[:].indirect(places[:]), h[:], wgs_t[:], ALU.mult)

        def add_base(engine, b, i, cols):
            page = pages[(PACK * b + i) % PAGES]
            engine.tensor_tensor(z[b][:, i, cols], page[:, cols], z[b][:, i, cols], ALU.add)

        def pair_tile():
            return ring.tile([P, 2, CHUNK * PACK], BF16, name="pair", tag="pair", bufs=3, align_bytes=64)

        def quantize_pair(pair):
            codes, scales = operand()
            nc.vector.quantize_mx(out=codes[:].bitcast(FP8X4), scales=scales[:],
                                  in_=pair[:].rearrange("p s n -> p (s n)"))
            return codes, scales

        def cells_by_vector(b, c, copy):
            cols = slice(c * CHUNK, (c + 1) * CHUNK)
            pair = pair_tile()
            source = z[b][:, :, cols].rearrange("p i (g e) -> p g i e", e=4)
            woven = [pair[:, s, :].rearrange("p (g e i) -> p g i e", e=4, i=PACK) for s in range(2)]
            copy(out=woven[0], in_=source)
            nc.scalar.activation(out=woven[1], in_=source, func=ACT.Square)
            return quantize_pair(pair)

        def cells_by_tensor(b, c):
            pair = pair_tile()
            words = pair[:].bitcast(F32)
            for k in range(CHUNK // P):
                block = c * (CHUNK // P) + k
                cols = slice(block * P, (block + 1) * P)
                summed = bank(block % 4, [P, PACK, P], "summed")
                for i in range(PACK):
                    for s, source in enumerate((z[b][:, i, cols], pages[(PACK * b + i) % PAGES][:, cols])):
                        nc.tensor.matmul(summed[:, i, :], lhsT=source, rhs=identity[:], is_transpose=True,
                                         start=(i == 0 and s == 0), stop=(i == PACK - 1 and s == 1))
                rounded = ring.tile([P, 2, 2, P, 2], BF16, name="cell_words", tag="cell_words", bufs=2, align_bytes=64)
                source = summed[:].rearrange("m (u e) p -> m u p e", e=2)
                nc.scalar.copy(out=rounded[:, 0], in_=source)
                nc.scalar.activation(out=rounded[:, 1], in_=source, func=ACT.Square)
                back = bank(4 + block % 4, [P, 2, 2, P], "back")
                as_words = rounded[:].rearrange("m s u p e -> m s u (p e)").bitcast(F32)
                for s in range(2):
                    for u in range(2):
                        nc.tensor.transpose(back[:, s, u, :], as_words[:, s, u, :], identity[:])
                nc.scalar.copy(out=words[:, :, k * 2 * P:(k + 1) * 2 * P].rearrange("p s (m u) -> p s m u", u=2),
                               in_=back[:].rearrange("p s u m -> p s m u"))
            return quantize_pair(pair)

        everything = slice(0, T2)
        wq_s = kept([P, PACK, P], U8, "wq_s")
        wq_w = [ring.tile([P, PACK, P], I32, name="wq_w", tag="wq%d" % g, align_bytes=64) for g in range(H_PASSES)]
        for g in range(H_PASSES):
            nc.vector.tensor_copy(out=wq_w[g][:].rearrange("p t m -> p m t"),
                                  in_=wq_raw[:, g, :].rearrange("p (m t) -> p m t", t=PACK))
        nc.vector.tensor_copy(out=wq_s[:].rearrange("p t m -> p m t"),
                              in_=wq_s_raw[:].rearrange("p (m t) -> p m t", t=PACK))
        z_q = {}
        for i in range(2):
            put(0, i, uplift(0, i))
        wc_q[0, 1] = quantize_weight(wc_raw[0, 1], False)
        wc_q[1, 1] = quantize_weight(wc_raw[1, 1], False)
        wc_q[2, 1] = quantize_weight(wc_raw[2, 1], False, shared[1])
        put(0, 2, uplift(0, 2, shared[0]))
        put(0, 3, uplift(0, 3, shared[1]))
        stage_one_second()
        hs = [uplift(1, i) for i in range(PACK)]
        wl_q = [quantize_weight(wl_raw[0], True, ("terms0", 1))]
        for i in range(PACK - 1):
            put(1, i, hs[i])
        for i in range(PACK - 1):
            add_base(nc.vector, 1, i, everything)
        for c in range(CHUNKS):
            z_q[0, c] = cells_by_tensor(0, c)
        put(1, PACK - 1, hs[PACK - 1])
        wl_q.append(quantize_weight(wl_raw[1], True, ("terms1", 1)))

        scores = [[bank(2 * c + u, [P, 2, CHUNK], "scores") for u in range(2)] for c in range(CHUNKS)]

        def stage_two(b, c):
            codes, scales = z_q[b, c]
            wl_c, wl_s = wl_q[b]
            for t in range(PACK):
                cols = slice(t * P, (t + 1) * P)
                stationary = [(wl_c[:, cols], wl_s[:, cols]), (wq_w[b][:, t, :], wq_s[4 * b:, t, :])]
                for s in range(2):
                    half = slice(s * CHUNK, (s + 1) * CHUNK)
                    nc.tensor.matmul_mx(
                        out=scores[c][t // 2][:, t % 2, :],
                        lhsT=stationary[s][0].bitcast(FP8X4), lhsT_scale=stationary[s][1],
                        rhs=codes[:, half].bitcast(FP8X4), rhs_scale=scales[:, half],
                        start=(b == 0 and t % 2 == 0 and s == 0),
                        stop=(b == H_PASSES - 1 and t % 2 == 1 and s == 1),
                    )

        for c in range(CHUNKS):
            stage_two(0, c)

        y_codes = kept([P, T2], U32, "y_codes")
        y_scales = kept([P, T2], U8, "y_scales")
        y_rows = out_0.rearrange("(p t) m -> p t m", t=PACK)
        code_rows = out_1[0].rearrange("p m t -> p (m t)").bitcast(I32)

        def finish(c):
            cols = slice(c * CHUNK, (c + 1) * CHUNK)
            y = raw_slot([P, PACK, CHUNK], "y", ("raw", 3) if c < 3 else shared[0])
            for u in range(2):
                nc.scalar.activation(out=y[:, 2 * u:2 * u + 2, :], in_=scores[c][u][:], func=ACT.Sigmoid)
            for t in range(PACK):
                if t < PACK - GAINS_ON_SCALAR:
                    nc.vector.tensor_scalar(y[:, t, :], y[:, t, :], gain_t[:, t:t + 1], None, ALU.mult)
                else:
                    nc.scalar.activation(out=y[:, t, :], in_=y[:, t, :], func=ACT.Copy, scale=gain_t[:, t:t + 1])
            nc.sync.dma_start(out=y_rows[:, :, cols], in_=y[:])
            rounded = ring.tile([P, PACK * CHUNK], BF16, name="y_rounded", tag="rounded", bufs=2, align_bytes=64)
            nc.vector.tensor_copy(out=rounded[:].rearrange("p (g e t) -> p g t e", e=4, t=PACK),
                                  in_=y[:].rearrange("p t (g e) -> p g t e", e=4))
            nc.vector.quantize_mx(out=y_codes[:, cols].bitcast(FP8X4), scales=y_scales[:, cols], in_=rounded[:])
            nc.sync.dma_start(out=code_rows[:, cols], in_=y_codes[:, cols].bitcast(I32))

        for c in range(CHUNKS):
            add_base(nc.vector, 1, PACK - 1, slice(c * CHUNK, (c + 1) * CHUNK))
            z_q[1, c] = cells_by_vector(1, c, nc.scalar.copy if c < ROUNDS_ON_SCALAR else nc.vector.tensor_copy)
            stage_two(1, c)
        for c in range(CHUNKS):
            finish(c)
        scale_rows = out_2[0].bitcast(I32).rearrange("(q r) n -> r q n", r=4)
        for r in range(4):
            nc.scalar.dma_start(out=scale_rows[r], in_=y_scales[:].bitcast(I32)[r:P:32])
